import numpy as np, ml_dtypes
CORES = [125,127,253,255,381,383,509,511]
N = 8
R = 64
def setup_inputs(rng):
    m = (rng.standard_normal((N, 128, 128), dtype=np.float32) / 11).astype(ml_dtypes.bfloat16)
    q = rng.standard_normal((128, R), dtype=np.float32).astype(ml_dtypes.bfloat16)
    return {"m": m, "mt": m.transpose(0, 2, 1).copy(), "q": np.broadcast_to(q, (N, 128, R)).copy()}
def setup_inputs_big(rng):
    d = setup_inputs(rng)
    for k in ("m", "mt", "q"): d[k] = (d[k].astype(np.float32) * 1024.0).astype(d[k].dtype)
    return d
def setup_inputs_small(rng):
    d = setup_inputs(rng)
    for k in ("m", "mt", "q"): d[k] = (d[k].astype(np.float32) * (1 / 1024.0)).astype(d[k].dtype)
    return d
def setup_inputs_apart(rng):
    d = setup_inputs(rng)
    f = (10.0 ** rng.permutation(np.linspace(-1.5, 1.5, N))).astype(np.float32).reshape(N, 1, 1)
    for k in ("m", "mt"): d[k] = (d[k].astype(np.float32) * f).astype(d[k].dtype)
    return d
def tie_inputs(x):
    x = dict(x)
    x["mt"] = x["m"].transpose(0, 2, 1).copy(); x["q"] = np.broadcast_to(x["q"][0], x["q"].shape).copy()
    return x
def reference(m, mt, q):
    M, MT, Q = m.astype(np.float64), mt.astype(np.float64), q.astype(np.float64)
    p = sum(MT[j].T @ Q[j] for j in range(N))
    q2 = sum(M[j].T @ p for j in range(N))
    return {"p": np.broadcast_to(p.astype(ml_dtypes.bfloat16 if m.dtype != np.float64 else np.float64), (N, 128, R)), "q2": np.broadcast_to(q2.astype(ml_dtypes.bfloat16 if m.dtype != np.float64 else np.float64), (N, 128, R))}

@@ -1,0 +1,115 @@
+from concourse.bass import DstId, RemoteDMATransfer
+from concourse.mybir import AluOpType
+
+K = 128
+R = 64
+W = K + R
+
+SCRATCH = {
+    "mt_s": ("sbuf", [128, K], "bfloat16"),
+    "q_s": ("sbuf", [128, R], "bfloat16"),
+    "d": ("sbuf", [128, W], "bfloat16"),
+    "lp": ("sbuf", [128, W], "bfloat16"),
+    "l0": ("sbuf", [128, W], "bfloat16"),
+    "l1": ("sbuf", [128, W], "bfloat16"),
+    "r": ("sbuf", [128, W], "bfloat16"),
+    "g1": ("sbuf", [128, W], "bfloat16"),
+    "g2": ("sbuf", [128, W], "bfloat16"),
+    "gs": ("sbuf", [128, W], "bfloat16"),
+    "p_s": ("sbuf", [128, R], "bfloat16"),
+    "q2_s": ("sbuf", [128, R], "bfloat16"),
+    "pj_ps": ("psum", [128, 512], "float32"),
+    "q2_ps": ("psum", [128, 512], "float32"),
+}
+SEMAPHORES = ["ld_a", "ld_m", "mm1", "cp1", "sent", "a0", "a1", "a2", "v1", "v2", "v3", "mm2", "vp", "vq", "st"]
+
+
+def _bits(mask):
+    return [b for b in range(mask.bit_length()) if (mask >> b) & 1]
+
+
+def _take(mask, n):
+    out = 0
+    for b in _bits(mask)[:n]:
+        out |= 1 << b
+    return out
+
+
+def rank_program(g, core, T, topo):
+    if T.rank_of(core) is None:
+        return
+    s = T.sem
+    ranks = list(T.cores)
+    mine = sorted(x for x in ranks if topo.host(x) == topo.host(core) and topo.chip(x) == topo.chip(core))
+    slot = mine.index(core)
+    peer = [x for x in mine if x != core][0]
+    far = sorted(x for x in ranks
+                 if topo.rack(topo.host(x)) != topo.rack(topo.host(core)) and topo.may_write(core, x))
+    near = sorted(x for x in ranks if topo.same_plane(core, x))[slot]
+
+    off = topo.mask(core, far[0]) & topo.mask(core, near)
+    n_off = len(_bits(off))
+    on = _take(topo.mask(core, peer) & ~off, n_off // len(far))
+    n_on = len(_bits(on))
+
+    def dst(x):
+        rid, pid = topo.addr(x, core)
+        return DstId(rid=rid, pnc=pid)
+
+    m_of = lambda t: t[:, 0:K]
+    p_of = lambda t: t[:, K:W]
+
+    g.sync.dma_start(T.mt_s[:], T.mt[:]).then_inc(s.ld_a, 16)
+    g.scalar.dma_start(T.q_s[:], T.q[:]).then_inc(s.ld_a, 16)
+    g.scalar.dma_start(m_of(T.d), T.m[:]).then_inc(s.ld_m, 16)
+
+    g.tensor.wait_ge(s.ld_a, 32)
+    g.tensor.matmul(T.pj_ps[:, 0:R], T.mt_s[:], T.q_s[:], start=True, stop=True).then_inc(s.mm1, 1)
+    g.vector.wait_ge(s.mm1, 1)
+    g.vector.tensor_copy(p_of(T.d), T.pj_ps[:, 0:R]).then_inc(s.cp1, 1)
+
+    land = T["l%d" % slot]
+    g.wait_ge(s.ld_m, 16)
+    g.wait_ge(s.cp1, 1)
+    g.remote_dma_fused([
+        RemoteDMATransfer(dst_ids=[dst(x) for x in far], dma_engine_mask=off, remote_sem=s.a1,
+                          srcs=[T.d[:]], dsts=[land[:] for _ in far], alu_op=0),
+        RemoteDMATransfer(dst_ids=[dst(peer)], dma_engine_mask=on, remote_sem=s.a0,
+                          srcs=[T.d[:]], dsts=[T.lp[:]], alu_op=0),
+    ], local_sem=s.sent)
+
+    g.wait_ge(s.a0, n_on)
+    g.wait_ge(s.a1, n_off * len(far))
+    g.remote_dma_fused([
+        RemoteDMATransfer(dst_ids=[dst(near)], dma_engine_mask=off, remote_sem=s.a2,
+                          srcs=[T.d[:], T.lp[:], T.l0[:], T.l1[:]], dsts=[T.r[:]], alu_op=1),
+    ], local_sem=s.sent)
+
+    g.vector.wait_ge(s.cp1, 1)
+    g.vector.wait_ge(s.ld_m, 16)
+    g.vector.wait_ge(s.a0, n_on)
+    g.vector.tensor_tensor(T.g1[:], T.d[:], T.lp[:], op=AluOpType.add).then_inc(s.v1, 1)
+    g.vector.wait_ge(s.v1, 1)
+    g.vector.wait_ge(s.a1, n_off * len(far))
+    g.vector.tensor_tensor(T.g2[:], T.g1[:], T.l0[:], op=AluOpType.add).then_inc(s.v2, 1)
+    g.vector.wait_ge(s.v2, 1)
+    g.vector.tensor_tensor(T.gs[:], T.g2[:], T.l1[:], op=AluOpType.add).then_inc(s.v3, 1)
+    g.tensor.wait_ge(s.v3, 1)
+    g.tensor.matmul(T.q2_ps[:, 0:R], m_of(T.gs), p_of(T.gs), start=True, stop=False)
+
+    g.tensor.wait_ge(s.a2, n_off)
+    g.tensor.matmul(T.q2_ps[:, 0:R], m_of(T.gs), p_of(T.r), start=False, stop=False)
+    g.tensor.matmul(T.q2_ps[:, 0:R], m_of(T.r), p_of(T.gs), start=False, stop=False)
+    g.tensor.matmul(T.q2_ps[:, 0:R], m_of(T.r), p_of(T.r), start=False, stop=True).then_inc(s.mm2, 1)
+    g.vector.wait_ge(s.v3, 1)
+    g.vector.wait_ge(s.a2, n_off)
+    g.vector.tensor_tensor(T.p_s[:], p_of(T.gs), p_of(T.r), op=AluOpType.add).then_inc(s.vp, 1)
+    g.sync.wait_ge(s.vp, 1)
+    g.sync.dma_start(T.p[:], T.p_s[:]).then_inc(s.st, 16)
+    g.vector.wait_ge(s.mm2, 1)
+    g.vector.tensor_copy(T.q2_s[:], T.q2_ps[:, 0:R]).then_inc(s.vq, 1)
+    g.scalar.wait_ge(s.vq, 1)
+    g.scalar.dma_start(T.q2[:], T.q2_s[:]).then_inc(s.st, 16)
+
+    g.wait_ge(s.sent, n_off + n_on + n_off)
+    g.wait_ge(s.st, 32)

@@ -3,25 +3,30 @@ from concourse.mybir import AluOpType
 
 K = 128
 R = 64
-W = K + R
 
 SCRATCH = {
-    "mt_s": ("sbuf", [128, K], "bfloat16"),
     "q_s": ("sbuf", [128, R], "bfloat16"),
-    "d": ("sbuf", [128, W], "bfloat16"),
-    "lp": ("sbuf", [128, W], "bfloat16"),
-    "l0": ("sbuf", [128, W], "bfloat16"),
-    "l1": ("sbuf", [128, W], "bfloat16"),
-    "r": ("sbuf", [128, W], "bfloat16"),
-    "g1": ("sbuf", [128, W], "bfloat16"),
-    "g2": ("sbuf", [128, W], "bfloat16"),
-    "gs": ("sbuf", [128, W], "bfloat16"),
+    "d": ("sbuf", [128, K], "bfloat16"),
+    "lp": ("sbuf", [128, K], "bfloat16"),
+    "l0": ("sbuf", [128, K], "bfloat16"),
+    "l1": ("sbuf", [128, K], "bfloat16"),
+    "r": ("sbuf", [128, K], "bfloat16"),
+    "coln": ("sbuf", [128, K], "bfloat16"),
+    "cst": ("sbuf", [128, K], "bfloat16"),
+    "one": ("sbuf", [128, K], "bfloat16"),
+    "e1": ("sbuf", [128, K], "bfloat16"),
+    "e2": ("sbuf", [128, K], "bfloat16"),
+    "e3": ("sbuf", [128, K], "bfloat16"),
+    "eye": ("sbuf", [128, K], "bfloat16"),
+    "s_s": ("sbuf", [128, K], "bfloat16"),
     "p_s": ("sbuf", [128, R], "bfloat16"),
     "q2_s": ("sbuf", [128, R], "bfloat16"),
-    "pj_ps": ("psum", [128, 512], "float32"),
+    "i_ps": ("psum", [128, 512], "float32"),
+    "p_ps": ("psum", [128, 512], "float32"),
+    "s_ps": ("psum", [128, 512], "float32"),
     "q2_ps": ("psum", [128, 512], "float32"),
 }
-SEMAPHORES = ["ld_a", "ld_m", "mm1", "cp1", "sent", "a0", "a1", "a2", "v1", "v2", "v3", "mm2", "vp", "vq", "st"]
+SEMAPHORES = ["ld_m", "ld_q", "vi", "mi", "sent", "a0", "a1", "a2", "mp", "ms", "vp", "vs", "mq", "vq", "st"]
 
 
 def _bits(mask):
@@ -39,75 +44,100 @@ def rank_program(g, core, T, topo):
     if T.rank_of(core) is None:
         return
     s = T.sem
+    v, te = g.vector, g.tensor
     ranks = list(T.cores)
     mine = sorted(x for x in ranks if topo.host(x) == topo.host(core) and topo.chip(x) == topo.chip(core))
     slot = mine.index(core)
     peer = [x for x in mine if x != core][0]
-    far = sorted(x for x in ranks
-                 if topo.rack(topo.host(x)) != topo.rack(topo.host(core)) and topo.may_write(core, x))
-    near = sorted(x for x in ranks if topo.same_plane(core, x))[slot]
+    plane = sorted(x for x in ranks if topo.same_plane(core, x))
+    cabled = sorted(x for x in ranks if topo.rack(topo.host(x)) != topo.rack(topo.host(core))
+                    and topo.may_write(core, x))[slot]
 
-    off = topo.mask(core, far[0]) & topo.mask(core, near)
+    off = topo.mask(core, plane[0]) & topo.mask(core, cabled)
     n_off = len(_bits(off))
-    on = _take(topo.mask(core, peer) & ~off, n_off // len(far))
+    on = _take(topo.mask(core, peer) & ~off, n_off // len(plane))
     n_on = len(_bits(on))
 
     def dst(x):
         rid, pid = topo.addr(x, core)
         return DstId(rid=rid, pnc=pid)
 
-    m_of = lambda t: t[:, 0:K]
-    p_of = lambda t: t[:, K:W]
-
-    g.sync.dma_start(T.mt_s[:], T.mt[:]).then_inc(s.ld_a, 16)
-    g.scalar.dma_start(T.q_s[:], T.q[:]).then_inc(s.ld_a, 16)
-    g.scalar.dma_start(m_of(T.d), T.m[:]).then_inc(s.ld_m, 16)
-
-    g.tensor.wait_ge(s.ld_a, 32)
-    g.tensor.matmul(T.pj_ps[:, 0:R], T.mt_s[:], T.q_s[:], start=True, stop=True).then_inc(s.mm1, 1)
-    g.vector.wait_ge(s.mm1, 1)
-    g.vector.tensor_copy(p_of(T.d), T.pj_ps[:, 0:R]).then_inc(s.cp1, 1)
+    g.sync.dma_start(T.d[:], T.mt[:]).then_inc(s.ld_m, 16)
+    g.scalar.dma_start(T.q_s[:], T.q[:]).then_inc(s.ld_q, 16)
 
     land = T["l%d" % slot]
     g.wait_ge(s.ld_m, 16)
-    g.wait_ge(s.cp1, 1)
     g.remote_dma_fused([
-        RemoteDMATransfer(dst_ids=[dst(x) for x in far], dma_engine_mask=off, remote_sem=s.a1,
-                          srcs=[T.d[:]], dsts=[land[:] for _ in far], alu_op=0),
+        RemoteDMATransfer(dst_ids=[dst(x) for x in plane], dma_engine_mask=off, remote_sem=s.a1,
+                          srcs=[T.d[:]], dsts=[land[:] for _ in plane], alu_op=0),
         RemoteDMATransfer(dst_ids=[dst(peer)], dma_engine_mask=on, remote_sem=s.a0,
                           srcs=[T.d[:]], dsts=[T.lp[:]], alu_op=0),
     ], local_sem=s.sent)
 
     g.wait_ge(s.a0, n_on)
-    g.wait_ge(s.a1, n_off * len(far))
+    g.wait_ge(s.a1, n_off * len(plane))
     g.remote_dma_fused([
-        RemoteDMATransfer(dst_ids=[dst(near)], dma_engine_mask=off, remote_sem=s.a2,
+        RemoteDMATransfer(dst_ids=[dst(cabled)], dma_engine_mask=off, remote_sem=s.a2,
                           srcs=[T.d[:], T.lp[:], T.l0[:], T.l1[:]], dsts=[T.r[:]], alu_op=1),
     ], local_sem=s.sent)
 
-    g.vector.wait_ge(s.cp1, 1)
-    g.vector.wait_ge(s.ld_m, 16)
-    g.vector.wait_ge(s.a0, n_on)
-    g.vector.tensor_tensor(T.g1[:], T.d[:], T.lp[:], op=AluOpType.add).then_inc(s.v1, 1)
-    g.vector.wait_ge(s.v1, 1)
-    g.vector.wait_ge(s.a1, n_off * len(far))
-    g.vector.tensor_tensor(T.g2[:], T.g1[:], T.l0[:], op=AluOpType.add).then_inc(s.v2, 1)
-    g.vector.wait_ge(s.v2, 1)
-    g.vector.tensor_tensor(T.gs[:], T.g2[:], T.l1[:], op=AluOpType.add).then_inc(s.v3, 1)
-    g.tensor.wait_ge(s.v3, 1)
-    g.tensor.matmul(T.q2_ps[:, 0:R], m_of(T.gs), p_of(T.gs), start=True, stop=False)
+    done = [0]
 
-    g.tensor.wait_ge(s.a2, n_off)
-    g.tensor.matmul(T.q2_ps[:, 0:R], m_of(T.gs), p_of(T.r), start=False, stop=False)
-    g.tensor.matmul(T.q2_ps[:, 0:R], m_of(T.r), p_of(T.gs), start=False, stop=False)
-    g.tensor.matmul(T.q2_ps[:, 0:R], m_of(T.r), p_of(T.r), start=False, stop=True).then_inc(s.mm2, 1)
-    g.vector.wait_ge(s.v3, 1)
-    g.vector.wait_ge(s.a2, n_off)
-    g.vector.tensor_tensor(T.p_s[:], p_of(T.gs), p_of(T.r), op=AluOpType.add).then_inc(s.vp, 1)
+    def vop(instr):
+        instr.then_inc(s.vi, 1)
+        done[0] += 1
+
+    vop(v.memset(T.coln[:, 0:1], 0.0))
+    vop(v.memset(T.one[:], 1.0))
+    step = 1
+    while step < K:
+        vop(v.memset(T.cst[:, step:2 * step], float(step)))
+        step *= 2
+    step = 1
+    while step < K:
+        v.wait_ge(s.vi, done[0])
+        vop(v.tensor_tensor(T.coln[:, step:2 * step], T.coln[:, 0:step], T.cst[:, step:2 * step], op=AluOpType.add))
+        step *= 2
+    te.wait_ge(s.vi, done[0])
+    te.matmul(T.i_ps[:, 0:K], T.coln[0:1, :], T.one[0:1, :], start=True, stop=True).then_inc(s.mi, 1)
+    v.wait_ge(s.vi, done[0])
+    v.wait_ge(s.mi, 1)
+    vop(v.tensor_tensor(T.e1[:], T.i_ps[:, 0:K], T.coln[:], op=AluOpType.subtract))
+    v.wait_ge(s.vi, done[0])
+    vop(v.tensor_tensor(T.e2[:], T.e1[:], T.e1[:], op=AluOpType.mult))
+    v.wait_ge(s.vi, done[0])
+    vop(v.tensor_tensor(T.e3[:], T.e2[:], T.one[:], op=AluOpType.min))
+    v.wait_ge(s.vi, done[0])
+    vop(v.tensor_tensor(T.eye[:], T.one[:], T.e3[:], op=AluOpType.subtract))
+
+    p_acc, s_acc = T.p_ps[:, 0:R], T.s_ps[:, 0:K]
+    te.wait_ge(s.ld_m, 16)
+    te.wait_ge(s.ld_q, 16)
+    te.wait_ge(s.vi, done[0])
+    te.matmul(p_acc, T.d[:], T.q_s[:], start=True, stop=False)
+    te.matmul(s_acc, T.d[:], T.eye[:], start=True, stop=False)
+    te.wait_ge(s.a0, n_on)
+    te.matmul(p_acc, T.lp[:], T.q_s[:], start=False, stop=False)
+    te.matmul(s_acc, T.lp[:], T.eye[:], start=False, stop=False)
+    te.wait_ge(s.a1, n_off * len(plane))
+    for t in (T.l0, T.l1):
+        te.matmul(p_acc, t[:], T.q_s[:], start=False, stop=False)
+        te.matmul(s_acc, t[:], T.eye[:], start=False, stop=False)
+    te.wait_ge(s.a2, n_off)
+    te.matmul(p_acc, T.r[:], T.q_s[:], start=False, stop=True).then_inc(s.mp, 1)
+    te.matmul(s_acc, T.r[:], T.eye[:], start=False, stop=True).then_inc(s.ms, 1)
+
+    v.wait_ge(s.mp, 1)
+    v.tensor_copy(T.p_s[:], p_acc).then_inc(s.vp, 1)
     g.sync.wait_ge(s.vp, 1)
     g.sync.dma_start(T.p[:], T.p_s[:]).then_inc(s.st, 16)
-    g.vector.wait_ge(s.mm2, 1)
-    g.vector.tensor_copy(T.q2_s[:], T.q2_ps[:, 0:R]).then_inc(s.vq, 1)
+    v.wait_ge(s.ms, 1)
+    v.tensor_copy(T.s_s[:], s_acc).then_inc(s.vs, 1)
+    te.wait_ge(s.vp, 1)
+    te.wait_ge(s.vs, 1)
+    te.matmul(T.q2_ps[:, 0:R], T.s_s[:], T.p_s[:], start=True, stop=True).then_inc(s.mq, 1)
+    v.wait_ge(s.mq, 1)
+    v.tensor_copy(T.q2_s[:], T.q2_ps[:, 0:R]).then_inc(s.vq, 1)
     g.scalar.wait_ge(s.vq, 1)
     g.scalar.dma_start(T.q2[:], T.q2_s[:]).then_inc(s.st, 16)
 

from concourse.bass import DstId, RemoteDMATransfer
from concourse.mybir import AluOpType

K = 128
R = 64

SCRATCH = {
    "q_s": ("sbuf", [128, R], "bfloat16"),
    "d": ("sbuf", [128, K], "bfloat16"),
    "lp": ("sbuf", [128, K], "bfloat16"),
    "l0": ("sbuf", [128, K], "bfloat16"),
    "l1": ("sbuf", [128, K], "bfloat16"),
    "r": ("sbuf", [128, K], "bfloat16"),
    "coln": ("sbuf", [128, K], "bfloat16"),
    "cst": ("sbuf", [128, K], "bfloat16"),
    "one": ("sbuf", [128, K], "bfloat16"),
    "e1": ("sbuf", [128, K], "bfloat16"),
    "e2": ("sbuf", [128, K], "bfloat16"),
    "e3": ("sbuf", [128, K], "bfloat16"),
    "eye": ("sbuf", [128, K], "bfloat16"),
    "s_s": ("sbuf", [128, K], "bfloat16"),
    "p_s": ("sbuf", [128, R], "bfloat16"),
    "q2_s": ("sbuf", [128, R], "bfloat16"),
    "i_ps": ("psum", [128, 512], "float32"),
    "p_ps": ("psum", [128, 512], "float32"),
    "s_ps": ("psum", [128, 512], "float32"),
    "q2_ps": ("psum", [128, 512], "float32"),
}
SEMAPHORES = ["ld_m", "ld_q", "vi", "mi", "sent", "a0", "a1", "a2", "mp", "ms", "vp", "vs", "mq", "vq", "st"]


def _bits(mask):
    return [b for b in range(mask.bit_length()) if (mask >> b) & 1]


def _take(mask, n):
    out = 0
    for b in _bits(mask)[:n]:
        out |= 1 << b
    return out


def rank_program(g, core, T, topo):
    if T.rank_of(core) is None:
        return
    s = T.sem
    v, te = g.vector, g.tensor
    ranks = list(T.cores)
    mine = sorted(x for x in ranks if topo.host(x) == topo.host(core) and topo.chip(x) == topo.chip(core))
    slot = mine.index(core)
    peer = [x for x in mine if x != core][0]
    plane = sorted(x for x in ranks if topo.same_plane(core, x))
    cabled = sorted(x for x in ranks if topo.rack(topo.host(x)) != topo.rack(topo.host(core))
                    and topo.may_write(core, x))[slot]

    off = topo.mask(core, plane[0]) & topo.mask(core, cabled)
    n_off = len(_bits(off))
    on = _take(topo.mask(core, peer) & ~off, n_off // len(plane))
    n_on = len(_bits(on))

    def dst(x):
        rid, pid = topo.addr(x, core)
        return DstId(rid=rid, pnc=pid)

    g.sync.dma_start(T.d[:], T.mt[:]).then_inc(s.ld_m, 16)
    g.scalar.dma_start(T.q_s[:], T.q[:]).then_inc(s.ld_q, 16)

    land = T["l%d" % slot]
    g.wait_ge(s.ld_m, 16)
    g.remote_dma_fused([
        RemoteDMATransfer(dst_ids=[dst(x) for x in plane], dma_engine_mask=off, remote_sem=s.a1,
                          srcs=[T.d[:]], dsts=[land[:] for _ in plane], alu_op=0),
        RemoteDMATransfer(dst_ids=[dst(peer)], dma_engine_mask=on, remote_sem=s.a0,
                          srcs=[T.d[:]], dsts=[T.lp[:]], alu_op=0),
    ], local_sem=s.sent)

    g.wait_ge(s.a0, n_on)
    g.wait_ge(s.a1, n_off * len(plane))
    g.remote_dma_fused([
        RemoteDMATransfer(dst_ids=[dst(cabled)], dma_engine_mask=off, remote_sem=s.a2,
                          srcs=[T.d[:], T.lp[:], T.l0[:], T.l1[:]], dsts=[T.r[:]], alu_op=1),
    ], local_sem=s.sent)

    done = [0]

    def vop(instr):
        instr.then_inc(s.vi, 1)
        done[0] += 1

    vop(v.memset(T.coln[:, 0:1], 0.0))
    vop(v.memset(T.one[:], 1.0))
    step = 1
    while step < K:
        vop(v.memset(T.cst[:, step:2 * step], float(step)))
        step *= 2
    step = 1
    while step < K:
        v.wait_ge(s.vi, done[0])
        vop(v.tensor_tensor(T.coln[:, step:2 * step], T.coln[:, 0:step], T.cst[:, step:2 * step], op=AluOpType.add))
        step *= 2
    te.wait_ge(s.vi, done[0])
    te.matmul(T.i_ps[:, 0:K], T.coln[0:1, :], T.one[0:1, :], start=True, stop=True).then_inc(s.mi, 1)
    v.wait_ge(s.vi, done[0])
    v.wait_ge(s.mi, 1)
    vop(v.tensor_tensor(T.e1[:], T.i_ps[:, 0:K], T.coln[:], op=AluOpType.subtract))
    v.wait_ge(s.vi, done[0])
    vop(v.tensor_tensor(T.e2[:], T.e1[:], T.e1[:], op=AluOpType.mult))
    v.wait_ge(s.vi, done[0])
    vop(v.tensor_tensor(T.e3[:], T.e2[:], T.one[:], op=AluOpType.min))
    v.wait_ge(s.vi, done[0])
    vop(v.tensor_tensor(T.eye[:], T.one[:], T.e3[:], op=AluOpType.subtract))

    p_acc, s_acc = T.p_ps[:, 0:R], T.s_ps[:, 0:K]
    te.wait_ge(s.ld_m, 16)
    te.wait_ge(s.ld_q, 16)
    te.wait_ge(s.vi, done[0])
    te.matmul(p_acc, T.d[:], T.q_s[:], start=True, stop=False)
    te.matmul(s_acc, T.d[:], T.eye[:], start=True, stop=False)
    te.wait_ge(s.a0, n_on)
    te.matmul(p_acc, T.lp[:], T.q_s[:], start=False, stop=False)
    te.matmul(s_acc, T.lp[:], T.eye[:], start=False, stop=False)
    te.wait_ge(s.a1, n_off * len(plane))
    for t in (T.l0, T.l1):
        te.matmul(p_acc, t[:], T.q_s[:], start=False, stop=False)
        te.matmul(s_acc, t[:], T.eye[:], start=False, stop=False)
    te.wait_ge(s.a2, n_off)
    te.matmul(p_acc, T.r[:], T.q_s[:], start=False, stop=True).then_inc(s.mp, 1)
    te.matmul(s_acc, T.r[:], T.eye[:], start=False, stop=True).then_inc(s.ms, 1)

    v.wait_ge(s.mp, 1)
    v.tensor_copy(T.p_s[:], p_acc).then_inc(s.vp, 1)
    g.sync.wait_ge(s.vp, 1)
    g.sync.dma_start(T.p[:], T.p_s[:]).then_inc(s.st, 16)
    v.wait_ge(s.ms, 1)
    v.tensor_copy(T.s_s[:], s_acc).then_inc(s.vs, 1)
    te.wait_ge(s.vp, 1)
    te.wait_ge(s.vs, 1)
    te.matmul(T.q2_ps[:, 0:R], T.s_s[:], T.p_s[:], start=True, stop=True).then_inc(s.mq, 1)
    v.wait_ge(s.mq, 1)
    v.tensor_copy(T.q2_s[:], T.q2_ps[:, 0:R]).then_inc(s.vq, 1)
    g.scalar.wait_ge(s.vq, 1)
    g.scalar.dma_start(T.q2[:], T.q2_s[:]).then_inc(s.st, 16)

    g.wait_ge(s.sent, n_off + n_on + n_off)
    g.wait_ge(s.st, 32)
